import numpy as np
import ml_dtypes


def mxq(x, axis, fmt="e4m3"):
    dtype, down = {"e4m3": (ml_dtypes.float8_e4m3fn, 7), "e5m2": (ml_dtypes.float8_e5m2, 14)}[fmt]
    v = np.moveaxis(np.asarray(x, np.float32).astype(ml_dtypes.bfloat16).astype(np.float64), axis, -1)
    blocks = v.reshape(v.shape[:-1] + (-1, 32))
    amax = np.abs(blocks).max(-1, keepdims=True)
    byte = np.maximum(np.where(amax > 0, np.frexp(amax)[1] - 1 + 127, 0) - down, 1)
    scale = np.exp2(byte - 127.0)
    codes = (blocks / scale).astype(np.float32).astype(dtype).astype(np.float64)
    return np.moveaxis((codes * scale).reshape(v.shape), -1, axis)


WIDE = False


def mx_kscale(k):
    if not WIDE:
        return np.ones(k)
    levels = np.array([10, -10, 5, -5, 0])
    if k % 512:
        return np.exp2(np.random.permutation(np.resize(levels, k // 32))).repeat(32)
    a = np.empty((k // 512, 16))
    for p in range(k // 512):
        a[p, :8] = np.random.permutation(np.resize(levels, 8))
        for g in range(8):
            far = levels[np.abs(levels - a[p, g]) >= 10]
            a[p, g + 8] = far[np.random.randint(len(far))]
    return np.exp2(a.ravel()).repeat(32)


def f64(x):
    return np.asarray(x).astype(np.float64)


E2M1 = np.array([0.0, 0.5, 1.0, 1.5, 2.0, 3.0, 4.0, 6.0, -0.0, -0.5, -1.0, -1.5, -2.0, -3.0, -4.0, -6.0])


def pack_weight(w, fmt):
    k, n = w.shape
    w = f64(np.asarray(w, np.float32).astype(ml_dtypes.bfloat16)).reshape(k // 32, 32, n)
    amax = np.abs(w).max(1)
    if fmt == "e4m3":
        byte = np.frexp(amax)[1] - 1 + 127 - 7
    else:
        mant, ex = np.frexp(amax / 6.0)
        byte = np.where(mant > 0.5, ex, ex - 1) + 127
    byte = np.clip(np.where(amax > 0, byte, 1), 1, 254)
    scaled = (w * np.exp2(127.0 - byte)[:, None, :]).reshape(k, n).astype(np.float32)
    by_word = np.ascontiguousarray(scaled.reshape(k // 512, 128, 4, n).transpose(0, 1, 3, 2))
    if fmt == "e4m3":
        words = by_word.astype(ml_dtypes.float8_e4m3fn).view(np.uint8)
    else:
        c = by_word.astype(ml_dtypes.float4_e2m1fn).view(np.uint8) & 0xF
        words = (c[..., 0::2] | (c[..., 1::2] << 4)).reshape(k // 512, 128, 2 * n)
    return np.ascontiguousarray(words), np.ascontiguousarray(byte.astype(np.uint8).reshape(k // 512, 16, n))


def unpack_weight(words, scales, fmt):
    g, _, n = scales.shape
    words = np.ascontiguousarray(words).reshape(g, 128, n, -1)
    if fmt == "e4m3":
        vals = words.view(ml_dtypes.float8_e4m3fn).astype(np.float64)
    else:
        nib = np.empty((g, 128, n, 4), np.uint8)
        nib[..., 0::2] = words & 0xF
        nib[..., 1::2] = words >> 4
        vals = E2M1[nib]
    vals = vals * np.repeat(np.exp2(scales.astype(np.float64) - 127.0), 8, axis=1)[..., None]
    return vals.transpose(0, 1, 3, 2).reshape(g * 512, n)


def bf(x):
    return np.asarray(x, np.float32).astype(ml_dtypes.bfloat16)


def planes(Y):
    r, m = Y.shape
    b = f64(bf(Y)).reshape(r // 32, 32, m)
    amax = np.abs(b).max(1)
    byte = np.clip(np.where(amax > 0, np.frexp(amax)[1] - 1 + 127 - 7, 1), 1, 254)
    codes = (b * np.exp2(127.0 - byte)[:, None, :]).reshape(r, m).astype(np.float32).astype(ml_dtypes.float8_e4m3fn).view(np.uint8)
    words = codes.reshape(r // 512, 128, 4, m).transpose(0, 1, 3, 2)
    return np.ascontiguousarray(words), np.ascontiguousarray(byte.astype(np.uint8).reshape(r // 512, 16, m))


K, L, T, N = 1024, 512, 512, 512


def setup_inputs():
    n = np.random.standard_normal
    fk = mx_kscale(K)
    fl = mx_kscale(L)
    wap = pack_weight(n((K, N)) * 1 / np.sqrt(K) * fk[:, None], "e2m1")
    xsp = pack_weight(n((L, T)) * np.random.uniform(0.3, 1.7, (1, T)) / fl[:, None], "e4m3")
    wsp = pack_weight(n((L, N)) * 1 / np.sqrt(L) * fl[:, None], "e2m1")
    wcp = pack_weight(n((K, N)) * 1 / np.sqrt(K) * fk[:, None], "e4m3")
    return {
        "xt": (n((K, T)) * np.random.uniform(0.3, 1.7, (1, T)) / fk[:, None]).astype(np.float32),
        "wa_words": wap[0],
        "wa_scales": wap[1],
        "xs_words": xsp[0],
        "xs_scales": xsp[1],
        "ws_words": wsp[0],
        "ws_scales": wsp[1],
        "wc_words": wcp[0],
        "wc_scales": wcp[1],
        "gm": (np.random.uniform(0.5, 2.0, (1, N))).astype(np.float32),
    }


def reference(xt, wa_words, wa_scales, xs_words, xs_scales, ws_words, ws_scales, wc_words, wc_scales, gm):
    wau = unpack_weight(wa_words, wa_scales, "e2m1")
    xsu = unpack_weight(xs_words, xs_scales, "e4m3")
    wsu = unpack_weight(ws_words, ws_scales, "e2m1")
    wcu = unpack_weight(wc_words, wc_scales, "e4m3")
    xtq = mxq(f64(xt), 0, "e4m3")
    a = xtq.T @ wau + xsu.T @ wsu
    b = xtq.T @ wcu
    ea = np.mean(np.square(a), axis=1, keepdims=True)
    eb = np.mean(np.square(b), axis=1, keepdims=True)
    y = (ea * a + eb * b) / (ea + eb + 0.01) * f64(gm)
    words, scales = planes(y)
    return y, words, scales

@@ -1,0 +1,256 @@
+from contextlib import ExitStack
+
+import concourse.mybir as mybir
+from concourse.masks import make_identity
+
+K, L, T, N = 1024, 512, 512, 512
+FLOPS = 2 * T * N * (2 * K + L)
+
+F32 = mybir.dt.float32
+BF16 = mybir.dt.bfloat16
+I32 = mybir.dt.int32
+U32 = mybir.dt.uint32
+U8 = mybir.dt.uint8
+FP8X4 = mybir.dt.float8_e4m3fn_x4
+FP4X4 = mybir.dt.float4_e2m1fn_x4
+ALU = mybir.AluOpType
+ACT = mybir.ActivationFunctionType
+
+P = 128
+PACK = 4
+QUADS = 4
+EPS = 0.01
+
+
+def tile_mix_rows_mixed_by_their_energy_pl_kernel(
+    tc, xt, wa_words, wa_scales, xs_words, xs_scales, ws_words, ws_scales, wc_words, wc_scales, gm, out_0, out_1, out_2
+):
+    nc = tc.nc
+    with ExitStack() as ctx:
+        sb = ctx.enter_context(tc.tile_pool(name="sb", bufs=1))
+        ps = ctx.enter_context(tc.psum_pool(name="ps", bufs=1))
+        ctx.enter_context(tc.manual_schedule())
+
+        def tile(name, shape, dtype):
+            return sb.tile(shape, dtype, name=name, align_bytes=64)
+
+        def bank(name):
+            return ps.tile([P, N], F32, name=name, tag=name)
+
+        def load_scale_rows(queue, plane, scales, quad):
+            queue.dma_start(
+                out=plane[32 * quad : 32 * quad + 4].bitcast(I32),
+                in_=scales[:, 4 * quad : 4 * quad + 4, :].rearrange("g r n -> r g n").bitcast(I32),
+            )
+
+        x_raw0 = tile("x_raw0", [P, PACK, T], F32)
+        x_raw1 = [tile("x_raw1_%d" % h, [P, PACK, T // 2], F32) for h in range(2)]
+        x_bf0 = tile("x_bf0", [P, PACK, P, PACK], BF16)
+        x_bf1 = [tile("x_bf1_%d" % h, [P, PACK, P // 2, PACK], BF16) for h in range(2)]
+        x_codes = [tile("x_codes%d" % g, [P, T], U32) for g in range(2)]
+        x_plane = [tile("x_plane%d" % g, [P, T], U8) for g in range(2)]
+        wc_codes = [tile("wc_codes%d" % g, [P, N], U32) for g in range(2)]
+        wa_codes = tile("wa_codes", [P, 2, 2 * N], U8)
+        ws_codes = tile("ws_codes", [P, 2 * N], U8)
+        xs_codes_raw = tile("xs_codes_raw", [P, T], U32)
+        xs_codes = tile("xs_codes", [P, T], U32)
+        wc_plane = tile("wc_plane", [P, 2, N], U8)
+        wa_plane = tile("wa_plane", [P, 2, N], U8)
+        ws_plane = tile("ws_plane", [P, 1, N], U8)
+        xs_plane_raw = tile("xs_plane_raw", [P, 1, T], U8)
+        xs_plane = tile("xs_plane", [P, T], U8)
+        gm_cols = tile("gm_cols", [P, PACK], F32)
+        gm_rows = tile("gm_rows", [P, N], F32)
+        ident = tile("ident", [P, P], F32)
+        warm = tile("warm", [P, 2], F32)
+        squares = [tile("squares%d" % i, [P, N], BF16) for i in range(2 * PACK)]
+        ea = tile("ea", [P, PACK], F32)
+        eb = tile("eb", [P, PACK], F32)
+        den = tile("den", [P, PACK], F32)
+        inv = tile("inv", [P, PACK], F32)
+        eb_b = [tile("eb_b%d" % r, [P, N], F32) for r in range(PACK)]
+        mix = [tile("mix%d" % r, [P, N], F32) for r in range(PACK)]
+        y = tile("y", [P, PACK, N], F32)
+        y_bf = tile("y_bf", [P, N, PACK], BF16)
+        y_codes = tile("y_codes", [P, N], U32)
+        y_plane = tile("y_plane", [P, N], U8)
+
+        nc.vector.memset(warm[:, 0:1], 0.0)
+        for plane in (wc_plane, wa_plane, ws_plane):
+            nc.vector.memset(plane[:].bitcast(I32), 0)
+        nc.scalar.activation(out=warm[:, 1:2], in_=warm[:, 0:1], func=ACT.Square)
+
+        nc.gpsimd.memset(xs_plane_raw[:].bitcast(I32), 0)
+        make_identity(nc, ident[:])
+        for quad in range(QUADS):
+            load_scale_rows(nc.gpsimd, xs_plane_raw, xs_scales, quad)
+
+        x_rows = xt.rearrange("(g p j) t -> g p j t", g=2, j=PACK)
+        words = lambda ap: ap.rearrange("p n t -> p (n t)").bitcast(I32)
+        nc.sync.dma_start(out=x_raw0[:], in_=x_rows[0])
+        for quad in range(QUADS):
+            load_scale_rows(nc.sync, wc_plane, wc_scales, quad)
+        nc.sync.dma_start(out=gm_cols[:], in_=gm.rearrange("o (p j) -> (o p) j", j=PACK))
+        nc.sync.dma_start(out=wc_codes[0][:].bitcast(I32), in_=words(wc_words[0]))
+        nc.sync.dma_start(out=x_raw1[0][:], in_=x_rows[1][:, :, 0 : T // 2])
+        nc.sync.dma_start(out=x_raw1[1][:], in_=x_rows[1][:, :, T // 2 : T])
+        for quad in range(QUADS):
+            load_scale_rows(nc.sync, wa_plane, wa_scales, quad)
+        for quad in range(1):
+            load_scale_rows(nc.sync, ws_plane, ws_scales, quad)
+        nc.sync.dma_start(out=wc_codes[1][:].bitcast(I32), in_=words(wc_words[1]))
+        nc.sync.dma_start(out=xs_codes_raw[:].bitcast(I32), in_=words(xs_words[0]))
+        nc.sync.dma_start(out=wa_codes[:].bitcast(I32), in_=wa_words.rearrange("g p c -> p g c").bitcast(I32))
+        for quad in range(1, QUADS):
+            load_scale_rows(nc.sync, ws_plane, ws_scales, quad)
+        nc.sync.dma_start(out=ws_codes[:].bitcast(I32), in_=ws_words[0].bitcast(I32))
+
+        gm_bank = bank("a3")
+        for j in range(PACK):
+            nc.tensor.transpose(gm_bank[:, j * P : (j + 1) * P], gm_cols[:, j : j + 1].to_broadcast([P, P]), ident[:])
+        nc.scalar.copy(
+            out=gm_rows[:].rearrange("p (n j) -> p n j", j=PACK), in_=gm_bank[:].rearrange("p (j n) -> p n j", j=PACK)
+        )
+
+        def deal(ap):
+            return ap.rearrange("p (r q) -> p q r", r=PACK)
+
+        def undealt(ap):
+            return ap.rearrange("p (q r) -> p q r", r=PACK)
+
+
+        def round_and_deal(raw, bf, vector_share):
+            src = raw[:].rearrange("p j (q r) -> p q j r", r=PACK)
+            dst = bf[:].rearrange("p r q j -> p q j r")
+            nc.vector.tensor_copy(out=dst[:, :vector_share], in_=src[:, :vector_share])
+            nc.scalar.copy(out=dst[:, vector_share:], in_=src[:, vector_share:])
+
+        round_and_deal(x_raw0, x_bf0, 80)
+        nc.vector.quantize_mx(
+            out=x_codes[0][:].bitcast(FP8X4), scales=x_plane[0][:], in_=x_bf0[:].rearrange("p r q j -> p (r q j)")
+        )
+
+        b = [bank("b%d" % r) for r in range(PACK)]
+        a = [bank("a%d" % r) for r in range(PACK)]
+
+        def tokens(r):
+            return slice(r * P, (r + 1) * P)
+
+        def b_pass(r, g):
+            nc.tensor.matmul_mx(
+                out=b[r][:], lhsT=x_codes[g][:, tokens(r)].bitcast(FP8X4), lhsT_scale=x_plane[g][:, tokens(r)],
+                rhs=wc_codes[g][:].bitcast(FP8X4), rhs_scale=wc_plane[:, g, :], start=(g == 0), stop=(g == 1),
+            )
+
+        def a_passes(r):
+            for g in range(2):
+                nc.tensor.matmul_mx(
+                    out=a[r][:], lhsT=x_codes[g][:, tokens(r)].bitcast(FP8X4), lhsT_scale=x_plane[g][:, tokens(r)],
+                    rhs=wa_codes[:, g, :].bitcast(FP4X4), rhs_scale=wa_plane[:, g, :], start=(g == 0), stop=False,
+                )
+            nc.tensor.matmul_mx(
+                out=a[r][:], lhsT=xs_codes[:, tokens(r)].bitcast(FP8X4), lhsT_scale=xs_plane[:, tokens(r)],
+                rhs=ws_codes[:].bitcast(FP4X4), rhs_scale=ws_plane[:, 0, :], start=False, stop=True,
+            )
+
+        for r in range(PACK):
+            b_pass(r, 0)
+
+        for h in range(2):
+            round_and_deal(x_raw1[h], x_bf1[h], 44)
+            for r in range(PACK):
+                cols = slice(r * P + h * 64, r * P + (h + 1) * 64)
+                nc.vector.quantize_mx(
+                    out=x_codes[1][:, cols].bitcast(FP8X4), scales=x_plane[1][:, cols],
+                    in_=x_bf1[h][:, r].rearrange("p q j -> p (q j)"),
+                )
+        nc.vector.tensor_copy(out=deal(xs_plane[:]), in_=undealt(xs_plane_raw[:, 0, :]))
+        nc.vector.tensor_copy(out=deal(xs_codes[:].bitcast(I32)), in_=undealt(xs_codes_raw[:].bitcast(I32)))
+
+        b_pass(0, 1)
+        b_pass(1, 1)
+        a_passes(0)
+        b_pass(2, 1)
+        a_passes(1)
+        a_passes(2)
+        b_pass(3, 1)
+        a_passes(3)
+
+        def energy(acc, e, r):
+            nc.scalar.activation(
+                out=squares.pop()[:], in_=acc[r][:], func=ACT.Square, scale=float(N) ** -0.5, accum_out=e[:, r : r + 1]
+            )
+
+        def weigh_b_vector(r):
+            nc.vector.tensor_scalar(out=eb_b[r][:], in0=b[r][:], scalar1=eb[:, r : r + 1], scalar2=None, op0=ALU.mult)
+
+        def weigh_b_scalar(r):
+            nc.scalar.activation(out=eb_b[r][:], in_=b[r][:], func=ACT.Copy, scale=eb[:, r : r + 1])
+
+        def mix_rows(r):
+            col = slice(r, r + 1)
+            nc.vector.tensor_scalar(
+                out=den[:, col], in0=ea[:, col], scalar1=eb[:, col], scalar2=EPS, op0=ALU.add, op1=ALU.add
+            )
+            nc.vector.scalar_tensor_tensor(
+                out=mix[r][:], in0=a[r][:], scalar=ea[:, col], in1=eb_b[r][:], op0=ALU.mult, op1=ALU.add
+            )
+            nc.vector.reciprocal(out=inv[:, col], in_=den[:, col])
+
+        y_rows = out_0.rearrange("(p r) n -> p r n", r=PACK)
+
+        def finish(r, cols):
+            nc.vector.scalar_tensor_tensor(
+                out=y[:, r, cols], in0=mix[r][:, cols], scalar=inv[:, r : r + 1], in1=gm_rows[:, cols],
+                op0=ALU.mult, op1=ALU.mult,
+            )
+
+        def store_y(r):
+            nc.sync.dma_start(out=y_rows[:, r, :], in_=y[:, r, :])
+
+        every = slice(0, N)
+        energy(b, eb, 0)
+        weigh_b_vector(0)
+        energy(b, eb, 1)
+        weigh_b_vector(1)
+        energy(a, ea, 0)
+        mix_rows(0)
+        energy(b, eb, 2)
+        finish(0, every)
+        store_y(0)
+        energy(a, ea, 1)
+        mix_rows(1)
+        weigh_b_scalar(2)
+        finish(1, every)
+        store_y(1)
+        energy(a, ea, 2)
+        mix_rows(2)
+        energy(b, eb, 3)
+        weigh_b_scalar(3)
+        finish(2, every)
+        store_y(2)
+        energy(a, ea, 3)
+        mix_rows(3)
+        finish(3, slice(0, N // 2))
+        finish(3, slice(N // 2, N))
+        store_y(3)
+
+        src = y[:].rearrange("p r (c i) -> p c r i", i=4)
+        dst = y_bf[:].rearrange("p (c i) r -> p c r i", i=4)
+        nc.scalar.copy(out=dst[:, 0:48], in_=src[:, 0:48])
+        nc.vector.tensor_copy(out=dst[:, 48:64], in_=src[:, 48:64])
+        nc.vector.tensor_copy(out=dst[:, 64:128], in_=src[:, 64:128])
+        out_words = words(out_1[0])
+        for h in range(2):
+            cols = slice(h * N // 2, (h + 1) * N // 2)
+            nc.vector.quantize_mx(
+                out=y_codes[:, cols].bitcast(FP8X4), scales=y_plane[:, cols],
+                in_=y_bf[:, cols, :].rearrange("p n r -> p (n r)"),
+            )
+            nc.sync.dma_start(out=out_words[:, cols], in_=y_codes[:, cols].bitcast(I32))
+        for quad in range(QUADS):
+            queue = nc.scalar if quad % 2 else nc.sync
+            queue.dma_start(
+                out=out_2[0, 4 * quad : 4 * quad + 4, :].bitcast(I32),
+                in_=y_plane[32 * quad : 32 * quad + 4, :].bitcast(I32),
+            )

@@ -37,9 +37,9 @@ def tile_mix_rows_mixed_by_their_energy_pl_kernel(
         def bank(name):
             return ps.tile([P, N], F32, name=name, tag=name)
 
-        def load_scale_rows(queue, plane, scales, quad):
+        def load_scale_rows(queue, plane, scales, quad, row=0):
             queue.dma_start(
-                out=plane[32 * quad : 32 * quad + 4].bitcast(I32),
+                out=plane[32 * quad + row : 32 * quad + row + 4].bitcast(I32),
                 in_=scales[:, 4 * quad : 4 * quad + 4, :].rearrange("g r n -> r g n").bitcast(I32),
             )
 
@@ -76,41 +76,38 @@ def tile_mix_rows_mixed_by_their_energy_pl_kernel(
         y_plane = tile("y_plane", [P, N], U8)
 
         nc.vector.memset(warm[:, 0:1], 0.0)
-        for plane in (wc_plane, wa_plane, ws_plane):
+        nc.vector.memset(ident[:], 0.0)
+        for plane in (ws_plane, wc_plane, xs_plane_raw, wa_plane):
             nc.vector.memset(plane[:].bitcast(I32), 0)
         nc.scalar.activation(out=warm[:, 1:2], in_=warm[:, 0:1], func=ACT.Square)
 
-        nc.gpsimd.memset(xs_plane_raw[:].bitcast(I32), 0)
-        make_identity(nc, ident[:])
-        for quad in range(QUADS):
-            load_scale_rows(nc.gpsimd, xs_plane_raw, xs_scales, quad)
+        nc.gpsimd.dma_start(out=gm_cols[:], in_=gm.rearrange("o (p j) -> (o p) j", j=PACK))
+        make_identity(nc, ident[:], nomemset=True)
+        for quad in range(3):
+            load_scale_rows(nc.gpsimd, ws_plane, ws_scales, quad)
 
         x_rows = xt.rearrange("(g p j) t -> g p j t", g=2, j=PACK)
         words = lambda ap: ap.rearrange("p n t -> p (n t)").bitcast(I32)
-        nc.sync.dma_start(out=x_raw0[:], in_=x_rows[0])
+        nc.sync.dma_start(out=x_raw0[:, 0:2], in_=x_rows[0][:, 0:2])
         for quad in range(QUADS):
-            load_scale_rows(nc.sync, wc_plane, wc_scales, quad)
-        nc.sync.dma_start(out=gm_cols[:], in_=gm.rearrange("o (p j) -> (o p) j", j=PACK))
+            load_scale_rows(nc.sync, wc_plane, wc_scales, quad, 4)
+        nc.sync.dma_start(out=x_raw0[:, 2:4], in_=x_rows[0][:, 2:4])
         nc.sync.dma_start(out=wc_codes[0][:].bitcast(I32), in_=words(wc_words[0]))
         nc.sync.dma_start(out=x_raw1[0][:], in_=x_rows[1][:, :, 0 : T // 2])
-        nc.sync.dma_start(out=x_raw1[1][:], in_=x_rows[1][:, :, T // 2 : T])
         for quad in range(QUADS):
-            load_scale_rows(nc.sync, wa_plane, wa_scales, quad)
-        for quad in range(1):
-            load_scale_rows(nc.sync, ws_plane, ws_scales, quad)
+            load_scale_rows(nc.sync, xs_plane_raw, xs_scales, quad)
+        nc.sync.dma_start(out=x_raw1[1][:], in_=x_rows[1][:, :, T // 2 : T])
         nc.sync.dma_start(out=wc_codes[1][:].bitcast(I32), in_=words(wc_words[1]))
         nc.sync.dma_start(out=xs_codes_raw[:].bitcast(I32), in_=words(xs_words[0]))
-        nc.sync.dma_start(out=wa_codes[:].bitcast(I32), in_=wa_words.rearrange("g p c -> p g c").bitcast(I32))
-        for quad in range(1, QUADS):
-            load_scale_rows(nc.sync, ws_plane, ws_scales, quad)
         nc.sync.dma_start(out=ws_codes[:].bitcast(I32), in_=ws_words[0].bitcast(I32))
+        load_scale_rows(nc.sync, ws_plane, ws_scales, 3)
+        nc.sync.dma_start(out=wa_codes[:].bitcast(I32), in_=wa_words.rearrange("g p c -> p g c").bitcast(I32))
+        for quad in range(QUADS):
+            load_scale_rows(nc.sync, wa_plane, wa_scales, quad)
 
         gm_bank = bank("a3")
         for j in range(PACK):
             nc.tensor.transpose(gm_bank[:, j * P : (j + 1) * P], gm_cols[:, j : j + 1].to_broadcast([P, P]), ident[:])
-        nc.scalar.copy(
-            out=gm_rows[:].rearrange("p (n j) -> p n j", j=PACK), in_=gm_bank[:].rearrange("p (j n) -> p n j", j=PACK)
-        )
 
         def deal(ap):
             return ap.rearrange("p (r q) -> p q r", r=PACK)
@@ -131,7 +128,6 @@ def tile_mix_rows_mixed_by_their_energy_pl_kernel(
         )
 
         b = [bank("b%d" % r) for r in range(PACK)]
-        a = [bank("a%d" % r) for r in range(PACK)]
 
         def tokens(r):
             return slice(r * P, (r + 1) * P)
@@ -139,19 +135,21 @@ def tile_mix_rows_mixed_by_their_energy_pl_kernel(
         def b_pass(r, g):
             nc.tensor.matmul_mx(
                 out=b[r][:], lhsT=x_codes[g][:, tokens(r)].bitcast(FP8X4), lhsT_scale=x_plane[g][:, tokens(r)],
-                rhs=wc_codes[g][:].bitcast(FP8X4), rhs_scale=wc_plane[:, g, :], start=(g == 0), stop=(g == 1),
+                rhs=wc_codes[g][:].bitcast(FP8X4), rhs_scale=wc_plane[4:, g, :], start=(g == 0), stop=(g == 1),
             )
 
-        def a_passes(r):
+        def a_second_input(r):
+            nc.tensor.matmul_mx(
+                out=a[r][:], lhsT=xs_codes[:, tokens(r)].bitcast(FP8X4), lhsT_scale=xs_plane[:, tokens(r)],
+                rhs=ws_codes[:].bitcast(FP4X4), rhs_scale=ws_plane[:, 0, :], start=True, stop=False,
+            )
+
+        def a_first_input(r):
             for g in range(2):
                 nc.tensor.matmul_mx(
                     out=a[r][:], lhsT=x_codes[g][:, tokens(r)].bitcast(FP8X4), lhsT_scale=x_plane[g][:, tokens(r)],
-                    rhs=wa_codes[:, g, :].bitcast(FP4X4), rhs_scale=wa_plane[:, g, :], start=(g == 0), stop=False,
+                    rhs=wa_codes[:, g, :].bitcast(FP4X4), rhs_scale=wa_plane[:, g, :], start=False, stop=(g == 1),
                 )
-            nc.tensor.matmul_mx(
-                out=a[r][:], lhsT=xs_codes[:, tokens(r)].bitcast(FP8X4), lhsT_scale=xs_plane[:, tokens(r)],
-                rhs=ws_codes[:].bitcast(FP4X4), rhs_scale=ws_plane[:, 0, :], start=False, stop=True,
-            )
 
         for r in range(PACK):
             b_pass(r, 0)
@@ -164,17 +162,23 @@ def tile_mix_rows_mixed_by_their_energy_pl_kernel(
                     out=x_codes[1][:, cols].bitcast(FP8X4), scales=x_plane[1][:, cols],
                     in_=x_bf1[h][:, r].rearrange("p q j -> p (q j)"),
                 )
-        nc.vector.tensor_copy(out=deal(xs_plane[:]), in_=undealt(xs_plane_raw[:, 0, :]))
+            if h == 0:
+                nc.vector.tensor_copy(out=deal(xs_plane[:]), in_=undealt(xs_plane_raw[:, 0, :]))
         nc.vector.tensor_copy(out=deal(xs_codes[:].bitcast(I32)), in_=undealt(xs_codes_raw[:].bitcast(I32)))
 
-        b_pass(0, 1)
-        b_pass(1, 1)
-        a_passes(0)
-        b_pass(2, 1)
-        a_passes(1)
-        a_passes(2)
-        b_pass(3, 1)
-        a_passes(3)
+        nc.scalar.copy(
+            out=gm_rows[:].rearrange("p (n j) -> p n j", j=PACK), in_=gm_bank[:].rearrange("p (j n) -> p n j", j=PACK)
+        )
+        a = [bank("a%d" % r) for r in range(PACK)]
+        for r in range(PACK):
+            b_pass(r, 1)
+        a_second_input(0)
+        a_second_input(1)
+        a_first_input(0)
+        a_first_input(1)
+        for r in range(2, PACK):
+            a_second_input(r)
+            a_first_input(r)
 
         def energy(acc, e, r):
             nc.scalar.activation(
@@ -209,28 +213,25 @@ def tile_mix_rows_mixed_by_their_energy_pl_kernel(
             nc.sync.dma_start(out=y_rows[:, r, :], in_=y[:, r, :])
 
         every = slice(0, N)
-        energy(b, eb, 0)
-        weigh_b_vector(0)
-        energy(b, eb, 1)
-        weigh_b_vector(1)
+        for r in range(3):
+            energy(b, eb, r)
+            weigh_b_vector(r)
         energy(a, ea, 0)
         mix_rows(0)
-        energy(b, eb, 2)
-        finish(0, every)
-        store_y(0)
         energy(a, ea, 1)
         mix_rows(1)
-        weigh_b_scalar(2)
+        energy(b, eb, 3)
+        finish(0, every)
+        store_y(0)
+        energy(a, ea, 2)
         finish(1, every)
         store_y(1)
-        energy(a, ea, 2)
         mix_rows(2)
-        energy(b, eb, 3)
         weigh_b_scalar(3)
-        finish(2, every)
-        store_y(2)
         energy(a, ea, 3)
         mix_rows(3)
+        finish(2, every)
+        store_y(2)
         finish(3, slice(0, N // 2))
         finish(3, slice(N // 2, N))
         store_y(3)

@@ -20,6 +20,7 @@ P = 128
 PACK = 4
 QUADS = 4
 EPS = 0.01
+VECTOR_SHARE = 46
 
 
 def tile_mix_rows_mixed_by_their_energy_pl_kernel(
@@ -43,10 +44,8 @@ def tile_mix_rows_mixed_by_their_energy_pl_kernel(
                 in_=scales[:, 4 * quad : 4 * quad + 4, :].rearrange("g r n -> r g n").bitcast(I32),
             )
 
-        x_raw0 = tile("x_raw0", [P, PACK, T], F32)
-        x_raw1 = [tile("x_raw1_%d" % h, [P, PACK, T // 2], F32) for h in range(2)]
-        x_bf0 = tile("x_bf0", [P, PACK, P, PACK], BF16)
-        x_bf1 = [tile("x_bf1_%d" % h, [P, PACK, P // 2, PACK], BF16) for h in range(2)]
+        x_raw = [[tile("x_raw%d%d" % (g, h), [P, PACK, T // 2], F32) for h in range(2)] for g in range(2)]
+        x_bf = [[tile("x_bf%d%d" % (g, h), [P, PACK, P // 2, PACK], BF16) for h in range(2)] for g in range(2)]
         x_codes = [tile("x_codes%d" % g, [P, T], U32) for g in range(2)]
         x_plane = [tile("x_plane%d" % g, [P, T], U8) for g in range(2)]
         wc_codes = [tile("wc_codes%d" % g, [P, N], U32) for g in range(2)]
@@ -76,34 +75,34 @@ def tile_mix_rows_mixed_by_their_energy_pl_kernel(
         y_plane = tile("y_plane", [P, N], U8)
 
         nc.vector.memset(warm[:, 0:1], 0.0)
-        nc.vector.memset(ident[:], 0.0)
-        for plane in (ws_plane, wc_plane, xs_plane_raw, wa_plane):
+        for plane in (wc_plane, xs_plane_raw, ws_plane):
             nc.vector.memset(plane[:].bitcast(I32), 0)
         nc.scalar.activation(out=warm[:, 1:2], in_=warm[:, 0:1], func=ACT.Square)
 
-        nc.gpsimd.dma_start(out=gm_cols[:], in_=gm.rearrange("o (p j) -> (o p) j", j=PACK))
-        make_identity(nc, ident[:], nomemset=True)
-        for quad in range(3):
-            load_scale_rows(nc.gpsimd, ws_plane, ws_scales, quad)
+        make_identity(nc, ident[:])
+        nc.gpsimd.memset(wa_plane[:].bitcast(I32), 0)
+        for quad in range(QUADS):
+            load_scale_rows(nc.gpsimd, wa_plane, wa_scales, quad)
 
         x_rows = xt.rearrange("(g p j) t -> g p j t", g=2, j=PACK)
         words = lambda ap: ap.rearrange("p n t -> p (n t)").bitcast(I32)
-        nc.sync.dma_start(out=x_raw0[:, 0:2], in_=x_rows[0][:, 0:2])
+        nc.sync.dma_start(out=gm_cols[:], in_=gm.rearrange("o (p j) -> (o p) j", j=PACK))
+        nc.sync.dma_start(out=x_raw[0][0][:], in_=x_rows[0][:, :, 0 : T // 2])
         for quad in range(QUADS):
             load_scale_rows(nc.sync, wc_plane, wc_scales, quad, 4)
-        nc.sync.dma_start(out=x_raw0[:, 2:4], in_=x_rows[0][:, 2:4])
+        nc.sync.dma_start(out=x_raw[0][1][:], in_=x_rows[0][:, :, T // 2 : T])
         nc.sync.dma_start(out=wc_codes[0][:].bitcast(I32), in_=words(wc_words[0]))
-        nc.sync.dma_start(out=x_raw1[0][:], in_=x_rows[1][:, :, 0 : T // 2])
+        nc.sync.dma_start(out=x_raw[1][0][:], in_=x_rows[1][:, :, 0 : T // 2])
         for quad in range(QUADS):
             load_scale_rows(nc.sync, xs_plane_raw, xs_scales, quad)
-        nc.sync.dma_start(out=x_raw1[1][:], in_=x_rows[1][:, :, T // 2 : T])
+        nc.sync.dma_start(out=x_raw[1][1][:], in_=x_rows[1][:, :, T // 2 : T])
         nc.sync.dma_start(out=wc_codes[1][:].bitcast(I32), in_=words(wc_words[1]))
         nc.sync.dma_start(out=xs_codes_raw[:].bitcast(I32), in_=words(xs_words[0]))
+        nc.sync.dma_start(out=wa_codes[:].bitcast(I32), in_=wa_words.rearrange("g p c -> p g c").bitcast(I32))
+        for quad in range(3):
+            load_scale_rows(nc.sync, ws_plane, ws_scales, quad)
         nc.sync.dma_start(out=ws_codes[:].bitcast(I32), in_=ws_words[0].bitcast(I32))
         load_scale_rows(nc.sync, ws_plane, ws_scales, 3)
-        nc.sync.dma_start(out=wa_codes[:].bitcast(I32), in_=wa_words.rearrange("g p c -> p g c").bitcast(I32))
-        for quad in range(QUADS):
-            load_scale_rows(nc.sync, wa_plane, wa_scales, quad)
 
         gm_bank = bank("a3")
         for j in range(PACK):
@@ -116,17 +115,20 @@ def tile_mix_rows_mixed_by_their_energy_pl_kernel(
             return ap.rearrange("p (q r) -> p q r", r=PACK)
 
 
-        def round_and_deal(raw, bf, vector_share):
-            src = raw[:].rearrange("p j (q r) -> p q j r", r=PACK)
-            dst = bf[:].rearrange("p r q j -> p q j r")
-            nc.vector.tensor_copy(out=dst[:, :vector_share], in_=src[:, :vector_share])
-            nc.scalar.copy(out=dst[:, vector_share:], in_=src[:, vector_share:])
+        def quantise_x(g, h):
+            src = x_raw[g][h][:].rearrange("p j (q r) -> p q r j", r=PACK)
+            dst = x_bf[g][h][:].rearrange("p r q j -> p q r j")
+            nc.vector.tensor_copy(out=dst[:, :VECTOR_SHARE], in_=src[:, :VECTOR_SHARE])
+            nc.scalar.copy(out=dst[:, VECTOR_SHARE:], in_=src[:, VECTOR_SHARE:])
+            for r in range(PACK):
+                cols = slice(r * P + h * 64, r * P + (h + 1) * 64)
+                nc.vector.quantize_mx(
+                    out=x_codes[g][:, cols].bitcast(FP8X4), scales=x_plane[g][:, cols],
+                    in_=x_bf[g][h][:, r].rearrange("p q j -> p (q j)"),
+                )
 
-        round_and_deal(x_raw0, x_bf0, 80)
-        nc.vector.quantize_mx(
-            out=x_codes[0][:].bitcast(FP8X4), scales=x_plane[0][:], in_=x_bf0[:].rearrange("p r q j -> p (r q j)")
-        )
-
+        quantise_x(0, 0)
+        quantise_x(0, 1)
         b = [bank("b%d" % r) for r in range(PACK)]
 
         def tokens(r):
@@ -141,44 +143,38 @@ def tile_mix_rows_mixed_by_their_energy_pl_kernel(
         def a_second_input(r):
             nc.tensor.matmul_mx(
                 out=a[r][:], lhsT=xs_codes[:, tokens(r)].bitcast(FP8X4), lhsT_scale=xs_plane[:, tokens(r)],
-                rhs=ws_codes[:].bitcast(FP4X4), rhs_scale=ws_plane[:, 0, :], start=True, stop=False,
+                rhs=ws_codes[:].bitcast(FP4X4), rhs_scale=ws_plane[:, 0, :], start=False, stop=True,
             )
 
         def a_first_input(r):
             for g in range(2):
                 nc.tensor.matmul_mx(
                     out=a[r][:], lhsT=x_codes[g][:, tokens(r)].bitcast(FP8X4), lhsT_scale=x_plane[g][:, tokens(r)],
-                    rhs=wa_codes[:, g, :].bitcast(FP4X4), rhs_scale=wa_plane[:, g, :], start=False, stop=(g == 1),
+                    rhs=wa_codes[:, g, :].bitcast(FP4X4), rhs_scale=wa_plane[:, g, :], start=(g == 0), stop=False,
                 )
 
         for r in range(PACK):
             b_pass(r, 0)
 
-        for h in range(2):
-            round_and_deal(x_raw1[h], x_bf1[h], 44)
-            for r in range(PACK):
-                cols = slice(r * P + h * 64, r * P + (h + 1) * 64)
-                nc.vector.quantize_mx(
-                    out=x_codes[1][:, cols].bitcast(FP8X4), scales=x_plane[1][:, cols],
-                    in_=x_bf1[h][:, r].rearrange("p q j -> p (q j)"),
-                )
-            if h == 0:
-                nc.vector.tensor_copy(out=deal(xs_plane[:]), in_=undealt(xs_plane_raw[:, 0, :]))
+        quantise_x(1, 0)
+        nc.vector.tensor_copy(
+            out=xs_plane[:].rearrange("p (r q) -> p r q", r=PACK),
+            in_=xs_plane_raw[:, 0, :].rearrange("p (q r) -> p r q", r=PACK),
+        )
+        quantise_x(1, 1)
         nc.vector.tensor_copy(out=deal(xs_codes[:].bitcast(I32)), in_=undealt(xs_codes_raw[:].bitcast(I32)))
 
         nc.scalar.copy(
             out=gm_rows[:].rearrange("p (n j) -> p n j", j=PACK), in_=gm_bank[:].rearrange("p (j n) -> p n j", j=PACK)
         )
         a = [bank("a%d" % r) for r in range(PACK)]
-        for r in range(PACK):
+        for r in range(3):
             b_pass(r, 1)
-        a_second_input(0)
-        a_second_input(1)
-        a_first_input(0)
-        a_first_input(1)
-        for r in range(2, PACK):
-            a_second_input(r)
+        for r in range(PACK):
             a_first_input(r)
+            a_second_input(r)
+            if r == 1:
+                b_pass(3, 1)
 
         def energy(acc, e, r):
             nc.scalar.activation(

@@ -19,8 +19,12 @@ ACT = mybir.ActivationFunctionType
 P = 128
 PACK = 4
 QUADS = 4
-EPS = 0.01
-VECTOR_SHARE = 46
+PASSES = K // (P * PACK)
+HALVES = 2
+HALF_Q = P // HALVES
+ROOT_EPS = 0.1
+VECTOR_Q = 46
+WC_ROW = 4
 
 
 def tile_mix_rows_mixed_by_their_energy_pl_kernel(
@@ -38,31 +42,40 @@ def tile_mix_rows_mixed_by_their_energy_pl_kernel(
         def bank(name):
             return ps.tile([P, N], F32, name=name, tag=name)
 
-        def load_scale_rows(queue, plane, scales, quad, row=0):
+        def words_as_int32(dram):
+            return dram.rearrange("p n j -> p (n j)").bitcast(I32)
+
+        def load_scale_rows(queue, plane, scales, quad, first_row=0):
+            row = 32 * quad + first_row
             queue.dma_start(
-                out=plane[32 * quad + row : 32 * quad + row + 4].bitcast(I32),
-                in_=scales[:, 4 * quad : 4 * quad + 4, :].rearrange("g r n -> r g n").bitcast(I32),
+                out=plane[row : row + 4].bitcast(I32),
+                in_=scales[:, 4 * quad : 4 * quad + 4, :].rearrange("g s n -> s g n").bitcast(I32),
             )
 
-        x_raw = [[tile("x_raw%d%d" % (g, h), [P, PACK, T // 2], F32) for h in range(2)] for g in range(2)]
-        x_bf = [[tile("x_bf%d%d" % (g, h), [P, PACK, P // 2, PACK], BF16) for h in range(2)] for g in range(2)]
-        x_codes = [tile("x_codes%d" % g, [P, T], U32) for g in range(2)]
-        x_plane = [tile("x_plane%d" % g, [P, T], U8) for g in range(2)]
-        wc_codes = [tile("wc_codes%d" % g, [P, N], U32) for g in range(2)]
-        wa_codes = tile("wa_codes", [P, 2, 2 * N], U8)
+        def hand(r):
+            return slice(r * P, (r + 1) * P)
+
+        x_raw = [[tile("x_raw%d%d" % (g, h), [P, PACK, T // HALVES], F32) for h in range(HALVES)] for g in range(PASSES)]
+        x_bf = [[tile("x_bf%d%d" % (g, h), [P, PACK, HALF_Q, PACK], BF16) for h in range(HALVES)] for g in range(PASSES)]
+        x_codes = [tile("x_codes%d" % g, [P, T], U32) for g in range(PASSES)]
+        x_plane = [tile("x_plane%d" % g, [P, T], U8) for g in range(PASSES)]
+        wc_codes = [tile("wc_codes%d" % g, [P, N], U32) for g in range(PASSES)]
+        wa_codes = tile("wa_codes", [P, PASSES, 2 * N], U8)
         ws_codes = tile("ws_codes", [P, 2 * N], U8)
         xs_codes_raw = tile("xs_codes_raw", [P, T], U32)
         xs_codes = tile("xs_codes", [P, T], U32)
-        wc_plane = tile("wc_plane", [P, 2, N], U8)
-        wa_plane = tile("wa_plane", [P, 2, N], U8)
+        wc_plane = tile("wc_plane", [P, PASSES, N], U8)
+        wa_plane = tile("wa_plane", [P, PASSES, N], U8)
         ws_plane = tile("ws_plane", [P, 1, N], U8)
         xs_plane_raw = tile("xs_plane_raw", [P, 1, T], U8)
         xs_plane = tile("xs_plane", [P, T], U8)
         gm_cols = tile("gm_cols", [P, PACK], F32)
         gm_rows = tile("gm_rows", [P, N], F32)
         ident = tile("ident", [P, P], F32)
-        warm = tile("warm", [P, 2], F32)
-        squares = [tile("squares%d" % i, [P, N], BF16) for i in range(2 * PACK)]
+        one = tile("one", [P, 1], F32)
+        eps = tile("eps", [P, 1], F32)
+        a_squares = [tile("a_squares%d" % r, [P, N], BF16) for r in range(PACK)]
+        b_squares = [tile("b_squares%d" % r, [P, N], BF16) for r in range(PACK)]
         ea = tile("ea", [P, PACK], F32)
         eb = tile("eb", [P, PACK], F32)
         den = tile("den", [P, PACK], F32)
@@ -74,174 +87,176 @@ def tile_mix_rows_mixed_by_their_energy_pl_kernel(
         y_codes = tile("y_codes", [P, N], U32)
         y_plane = tile("y_plane", [P, N], U8)
 
-        nc.vector.memset(warm[:, 0:1], 0.0)
+        nc.vector.memset(one[:], 1.0)
         for plane in (wc_plane, xs_plane_raw, ws_plane):
             nc.vector.memset(plane[:].bitcast(I32), 0)
-        nc.scalar.activation(out=warm[:, 1:2], in_=warm[:, 0:1], func=ACT.Square)
+        nc.scalar.activation(out=eps[:], in_=one[:], func=ACT.Square, scale=ROOT_EPS)
 
         make_identity(nc, ident[:])
         nc.gpsimd.memset(wa_plane[:].bitcast(I32), 0)
         for quad in range(QUADS):
             load_scale_rows(nc.gpsimd, wa_plane, wa_scales, quad)
 
-        x_rows = xt.rearrange("(g p j) t -> g p j t", g=2, j=PACK)
-        words = lambda ap: ap.rearrange("p n t -> p (n t)").bitcast(I32)
+        x_rows = xt.rearrange("(g p j) (h t) -> g h p j t", g=PASSES, j=PACK, h=HALVES)
         nc.sync.dma_start(out=gm_cols[:], in_=gm.rearrange("o (p j) -> (o p) j", j=PACK))
-        nc.sync.dma_start(out=x_raw[0][0][:], in_=x_rows[0][:, :, 0 : T // 2])
+        nc.sync.dma_start(out=x_raw[0][0][:], in_=x_rows[0, 0])
         for quad in range(QUADS):
-            load_scale_rows(nc.sync, wc_plane, wc_scales, quad, 4)
-        nc.sync.dma_start(out=x_raw[0][1][:], in_=x_rows[0][:, :, T // 2 : T])
-        nc.sync.dma_start(out=wc_codes[0][:].bitcast(I32), in_=words(wc_words[0]))
-        nc.sync.dma_start(out=x_raw[1][0][:], in_=x_rows[1][:, :, 0 : T // 2])
+            load_scale_rows(nc.sync, wc_plane, wc_scales, quad, WC_ROW)
+        nc.sync.dma_start(out=x_raw[0][1][:], in_=x_rows[0, 1])
+        nc.sync.dma_start(out=wc_codes[0][:].bitcast(I32), in_=words_as_int32(wc_words[0]))
+        nc.sync.dma_start(out=x_raw[1][0][:], in_=x_rows[1, 0])
         for quad in range(QUADS):
             load_scale_rows(nc.sync, xs_plane_raw, xs_scales, quad)
-        nc.sync.dma_start(out=x_raw[1][1][:], in_=x_rows[1][:, :, T // 2 : T])
-        nc.sync.dma_start(out=wc_codes[1][:].bitcast(I32), in_=words(wc_words[1]))
-        nc.sync.dma_start(out=xs_codes_raw[:].bitcast(I32), in_=words(xs_words[0]))
+        nc.sync.dma_start(out=x_raw[1][1][:], in_=x_rows[1, 1])
+        nc.sync.dma_start(out=wc_codes[1][:].bitcast(I32), in_=words_as_int32(wc_words[1]))
+        nc.sync.dma_start(out=xs_codes_raw[:].bitcast(I32), in_=words_as_int32(xs_words[0]))
         nc.sync.dma_start(out=wa_codes[:].bitcast(I32), in_=wa_words.rearrange("g p c -> p g c").bitcast(I32))
-        for quad in range(3):
+        for quad in range(QUADS - 1):
             load_scale_rows(nc.sync, ws_plane, ws_scales, quad)
         nc.sync.dma_start(out=ws_codes[:].bitcast(I32), in_=ws_words[0].bitcast(I32))
-        load_scale_rows(nc.sync, ws_plane, ws_scales, 3)
+        load_scale_rows(nc.sync, ws_plane, ws_scales, QUADS - 1)
 
-        gm_bank = bank("a3")
+        gm_bank = bank("a%d" % (PACK - 1))
         for j in range(PACK):
             nc.tensor.transpose(gm_bank[:, j * P : (j + 1) * P], gm_cols[:, j : j + 1].to_broadcast([P, P]), ident[:])
-
-        def deal(ap):
-            return ap.rearrange("p (r q) -> p q r", r=PACK)
-
-        def undealt(ap):
-            return ap.rearrange("p (q r) -> p q r", r=PACK)
-
 
         def quantise_x(g, h):
             src = x_raw[g][h][:].rearrange("p j (q r) -> p q r j", r=PACK)
             dst = x_bf[g][h][:].rearrange("p r q j -> p q r j")
-            nc.vector.tensor_copy(out=dst[:, :VECTOR_SHARE], in_=src[:, :VECTOR_SHARE])
-            nc.scalar.copy(out=dst[:, VECTOR_SHARE:], in_=src[:, VECTOR_SHARE:])
+            nc.vector.tensor_copy(out=dst[:, :VECTOR_Q], in_=src[:, :VECTOR_Q])
+            nc.scalar.copy(out=dst[:, VECTOR_Q:], in_=src[:, VECTOR_Q:])
             for r in range(PACK):
-                cols = slice(r * P + h * 64, r * P + (h + 1) * 64)
+                cols = slice(r * P + h * HALF_Q, r * P + (h + 1) * HALF_Q)
                 nc.vector.quantize_mx(
-                    out=x_codes[g][:, cols].bitcast(FP8X4), scales=x_plane[g][:, cols],
+                    out=x_codes[g][:, cols].bitcast(FP8X4),
+                    scales=x_plane[g][:, cols],
                     in_=x_bf[g][h][:, r].rearrange("p q j -> p (q j)"),
                 )
 
-        quantise_x(0, 0)
-        quantise_x(0, 1)
         b = [bank("b%d" % r) for r in range(PACK)]
-
-        def tokens(r):
-            return slice(r * P, (r + 1) * P)
 
         def b_pass(r, g):
             nc.tensor.matmul_mx(
-                out=b[r][:], lhsT=x_codes[g][:, tokens(r)].bitcast(FP8X4), lhsT_scale=x_plane[g][:, tokens(r)],
-                rhs=wc_codes[g][:].bitcast(FP8X4), rhs_scale=wc_plane[4:, g, :], start=(g == 0), stop=(g == 1),
+                out=b[r][:],
+                lhsT=x_codes[g][:, hand(r)].bitcast(FP8X4),
+                lhsT_scale=x_plane[g][:, hand(r)],
+                rhs=wc_codes[g][:].bitcast(FP8X4),
+                rhs_scale=wc_plane[WC_ROW:, g, :],
+                start=(g == 0),
+                stop=(g == PASSES - 1),
             )
 
-        def a_second_input(r):
-            nc.tensor.matmul_mx(
-                out=a[r][:], lhsT=xs_codes[:, tokens(r)].bitcast(FP8X4), lhsT_scale=xs_plane[:, tokens(r)],
-                rhs=ws_codes[:].bitcast(FP4X4), rhs_scale=ws_plane[:, 0, :], start=False, stop=True,
-            )
-
-        def a_first_input(r):
-            for g in range(2):
-                nc.tensor.matmul_mx(
-                    out=a[r][:], lhsT=x_codes[g][:, tokens(r)].bitcast(FP8X4), lhsT_scale=x_plane[g][:, tokens(r)],
-                    rhs=wa_codes[:, g, :].bitcast(FP4X4), rhs_scale=wa_plane[:, g, :], start=(g == 0), stop=False,
-                )
-
+        for h in range(HALVES):
+            quantise_x(0, h)
         for r in range(PACK):
             b_pass(r, 0)
+        for h in range(HALVES):
+            quantise_x(1, h)
 
-        quantise_x(1, 0)
         nc.vector.tensor_copy(
             out=xs_plane[:].rearrange("p (r q) -> p r q", r=PACK),
             in_=xs_plane_raw[:, 0, :].rearrange("p (q r) -> p r q", r=PACK),
         )
-        quantise_x(1, 1)
-        nc.vector.tensor_copy(out=deal(xs_codes[:].bitcast(I32)), in_=undealt(xs_codes_raw[:].bitcast(I32)))
-
-        nc.scalar.copy(
-            out=gm_rows[:].rearrange("p (n j) -> p n j", j=PACK), in_=gm_bank[:].rearrange("p (j n) -> p n j", j=PACK)
+        nc.vector.tensor_copy(
+            out=xs_codes[:].bitcast(I32).rearrange("p (r q) -> p q r", r=PACK),
+            in_=xs_codes_raw[:].bitcast(I32).rearrange("p (q r) -> p q r", r=PACK),
         )
-        a = [bank("a%d" % r) for r in range(PACK)]
-        for r in range(3):
-            b_pass(r, 1)
-        for r in range(PACK):
-            a_first_input(r)
-            a_second_input(r)
-            if r == 1:
-                b_pass(3, 1)
+        nc.scalar.copy(
+            out=gm_rows[:].rearrange("p (c j) -> p c j", j=PACK), in_=gm_bank[:].rearrange("p (j c) -> p c j", j=PACK)
+        )
 
-        def energy(acc, e, r):
-            nc.scalar.activation(
-                out=squares.pop()[:], in_=acc[r][:], func=ACT.Square, scale=float(N) ** -0.5, accum_out=e[:, r : r + 1]
+        a = [bank("a%d" % r) for r in range(PACK)]
+
+        def a_passes(r):
+            for g in range(PASSES):
+                nc.tensor.matmul_mx(
+                    out=a[r][:],
+                    lhsT=x_codes[g][:, hand(r)].bitcast(FP8X4),
+                    lhsT_scale=x_plane[g][:, hand(r)],
+                    rhs=wa_codes[:, g, :].bitcast(FP4X4),
+                    rhs_scale=wa_plane[:, g, :],
+                    start=(g == 0),
+                    stop=False,
+                )
+            nc.tensor.matmul_mx(
+                out=a[r][:],
+                lhsT=xs_codes[:, hand(r)].bitcast(FP8X4),
+                lhsT_scale=xs_plane[:, hand(r)],
+                rhs=ws_codes[:].bitcast(FP4X4),
+                rhs_scale=ws_plane[:, 0, :],
+                start=False,
+                stop=True,
             )
 
-        def weigh_b_vector(r):
-            nc.vector.tensor_scalar(out=eb_b[r][:], in0=b[r][:], scalar1=eb[:, r : r + 1], scalar2=None, op0=ALU.mult)
+        for r in (0, 1, 2):
+            b_pass(r, 1)
+        for r in (0, 1):
+            a_passes(r)
+        b_pass(3, 1)
+        for r in (2, 3):
+            a_passes(r)
 
-        def weigh_b_scalar(r):
-            nc.scalar.activation(out=eb_b[r][:], in_=b[r][:], func=ACT.Copy, scale=eb[:, r : r + 1])
+        def energy(acc, squares, e, r):
+            nc.scalar.activation(
+                out=squares[r][:], in_=acc[r][:], func=ACT.Square, scale=float(N) ** -0.5, accum_out=e[:, r : r + 1]
+            )
 
         def mix_rows(r):
             col = slice(r, r + 1)
             nc.vector.tensor_scalar(
-                out=den[:, col], in0=ea[:, col], scalar1=eb[:, col], scalar2=EPS, op0=ALU.add, op1=ALU.add
+                out=den[:, col], in0=ea[:, col], scalar1=eb[:, col], scalar2=eps[:], op0=ALU.add, op1=ALU.add
             )
             nc.vector.scalar_tensor_tensor(
                 out=mix[r][:], in0=a[r][:], scalar=ea[:, col], in1=eb_b[r][:], op0=ALU.mult, op1=ALU.add
             )
             nc.vector.reciprocal(out=inv[:, col], in_=den[:, col])
 
-        y_rows = out_0.rearrange("(p r) n -> p r n", r=PACK)
-
         def finish(r, cols):
             nc.vector.scalar_tensor_tensor(
-                out=y[:, r, cols], in0=mix[r][:, cols], scalar=inv[:, r : r + 1], in1=gm_rows[:, cols],
-                op0=ALU.mult, op1=ALU.mult,
+                out=y[:, r, cols],
+                in0=mix[r][:, cols],
+                scalar=inv[:, r : r + 1],
+                in1=gm_rows[:, cols],
+                op0=ALU.mult,
+                op1=ALU.mult,
             )
 
-        def store_y(r):
+        def round_pair(copy, first_hand, cols):
+            hands = slice(first_hand, first_hand + 2)
+            copy(out=y_bf[:, cols, hands], in_=y[:, hands, cols].rearrange("p r n -> p n r"))
+
+        y_rows = out_0.rearrange("(q r) n -> q r n", r=PACK)
+        all_cols = slice(0, N)
+        col_halves = (slice(0, N // 2), slice(N // 2, N))
+
+        for r in (0, 1, 2):
+            energy(b, b_squares, eb, r)
+            nc.vector.tensor_scalar(out=eb_b[r][:], in0=b[r][:], scalar1=eb[:, r : r + 1], scalar2=None, op0=ALU.mult)
+        for r in (0, 1):
+            energy(a, a_squares, ea, r)
+            mix_rows(r)
+        energy(b, b_squares, eb, 3)
+        energy(a, a_squares, ea, 2)
+        for r in (0, 1):
+            finish(r, all_cols)
             nc.sync.dma_start(out=y_rows[:, r, :], in_=y[:, r, :])
-
-        every = slice(0, N)
-        for r in range(3):
-            energy(b, eb, r)
-            weigh_b_vector(r)
-        energy(a, ea, 0)
-        mix_rows(0)
-        energy(a, ea, 1)
-        mix_rows(1)
-        energy(b, eb, 3)
-        finish(0, every)
-        store_y(0)
-        energy(a, ea, 2)
-        finish(1, every)
-        store_y(1)
         mix_rows(2)
-        weigh_b_scalar(3)
-        energy(a, ea, 3)
+        nc.scalar.activation(out=eb_b[3][:], in_=b[3][:], func=ACT.Copy, scale=eb[:, 3:4])
+        energy(a, a_squares, ea, 3)
         mix_rows(3)
-        finish(2, every)
-        store_y(2)
-        finish(3, slice(0, N // 2))
-        finish(3, slice(N // 2, N))
-        store_y(3)
+        round_pair(nc.scalar.copy, 0, all_cols)
+        for cols in col_halves:
+            finish(2, cols)
+            finish(3, cols)
+            nc.sync.dma_start(out=y_rows[:, 2:4, cols], in_=y[:, 2:4, cols])
+        round_pair(nc.scalar.copy, 2, col_halves[0])
+        round_pair(nc.vector.tensor_copy, 2, col_halves[1])
 
-        src = y[:].rearrange("p r (c i) -> p c r i", i=4)
-        dst = y_bf[:].rearrange("p (c i) r -> p c r i", i=4)
-        nc.scalar.copy(out=dst[:, 0:48], in_=src[:, 0:48])
-        nc.vector.tensor_copy(out=dst[:, 48:64], in_=src[:, 48:64])
-        nc.vector.tensor_copy(out=dst[:, 64:128], in_=src[:, 64:128])
-        out_words = words(out_1[0])
-        for h in range(2):
-            cols = slice(h * N // 2, (h + 1) * N // 2)
+        out_words = words_as_int32(out_1[0])
+        for cols in col_halves:
             nc.vector.quantize_mx(
-                out=y_codes[:, cols].bitcast(FP8X4), scales=y_plane[:, cols],
+                out=y_codes[:, cols].bitcast(FP8X4),
+                scales=y_plane[:, cols],
                 in_=y_bf[:, cols, :].rearrange("p n r -> p (n r)"),
             )
             nc.sync.dma_start(out=out_words[:, cols], in_=y_codes[:, cols].bitcast(I32))

from contextlib import ExitStack

import concourse.mybir as mybir
from concourse.masks import make_identity

K, L, T, N = 1024, 512, 512, 512
FLOPS = 2 * T * N * (2 * K + L)

F32 = mybir.dt.float32
BF16 = mybir.dt.bfloat16
I32 = mybir.dt.int32
U32 = mybir.dt.uint32
U8 = mybir.dt.uint8
FP8X4 = mybir.dt.float8_e4m3fn_x4
FP4X4 = mybir.dt.float4_e2m1fn_x4
ALU = mybir.AluOpType
ACT = mybir.ActivationFunctionType

P = 128
PACK = 4
QUADS = 4
PASSES = K // (P * PACK)
HALVES = 2
HALF_Q = P // HALVES
ROOT_EPS = 0.1
VECTOR_Q = 46
WC_ROW = 4


def tile_mix_rows_mixed_by_their_energy_pl_kernel(
    tc, xt, wa_words, wa_scales, xs_words, xs_scales, ws_words, ws_scales, wc_words, wc_scales, gm, out_0, out_1, out_2
):
    nc = tc.nc
    with ExitStack() as ctx:
        sb = ctx.enter_context(tc.tile_pool(name="sb", bufs=1))
        ps = ctx.enter_context(tc.psum_pool(name="ps", bufs=1))
        ctx.enter_context(tc.manual_schedule())

        def tile(name, shape, dtype):
            return sb.tile(shape, dtype, name=name, align_bytes=64)

        def bank(name):
            return ps.tile([P, N], F32, name=name, tag=name)

        def words_as_int32(dram):
            return dram.rearrange("p n j -> p (n j)").bitcast(I32)

        def load_scale_rows(queue, plane, scales, quad, first_row=0):
            row = 32 * quad + first_row
            queue.dma_start(
                out=plane[row : row + 4].bitcast(I32),
                in_=scales[:, 4 * quad : 4 * quad + 4, :].rearrange("g s n -> s g n").bitcast(I32),
            )

        def hand(r):
            return slice(r * P, (r + 1) * P)

        x_raw = [[tile("x_raw%d%d" % (g, h), [P, PACK, T // HALVES], F32) for h in range(HALVES)] for g in range(PASSES)]
        x_bf = [[tile("x_bf%d%d" % (g, h), [P, PACK, HALF_Q, PACK], BF16) for h in range(HALVES)] for g in range(PASSES)]
        x_codes = [tile("x_codes%d" % g, [P, T], U32) for g in range(PASSES)]
        x_plane = [tile("x_plane%d" % g, [P, T], U8) for g in range(PASSES)]
        wc_codes = [tile("wc_codes%d" % g, [P, N], U32) for g in range(PASSES)]
        wa_codes = tile("wa_codes", [P, PASSES, 2 * N], U8)
        ws_codes = tile("ws_codes", [P, 2 * N], U8)
        xs_codes_raw = tile("xs_codes_raw", [P, T], U32)
        xs_codes = tile("xs_codes", [P, T], U32)
        wc_plane = tile("wc_plane", [P, PASSES, N], U8)
        wa_plane = tile("wa_plane", [P, PASSES, N], U8)
        ws_plane = tile("ws_plane", [P, 1, N], U8)
        xs_plane_raw = tile("xs_plane_raw", [P, 1, T], U8)
        xs_plane = tile("xs_plane", [P, T], U8)
        gm_cols = tile("gm_cols", [P, PACK], F32)
        gm_rows = tile("gm_rows", [P, N], F32)
        ident = tile("ident", [P, P], F32)
        one = tile("one", [P, 1], F32)
        eps = tile("eps", [P, 1], F32)
        a_squares = [tile("a_squares%d" % r, [P, N], BF16) for r in range(PACK)]
        b_squares = [tile("b_squares%d" % r, [P, N], BF16) for r in range(PACK)]
        ea = tile("ea", [P, PACK], F32)
        eb = tile("eb", [P, PACK], F32)
        den = tile("den", [P, PACK], F32)
        inv = tile("inv", [P, PACK], F32)
        eb_b = [tile("eb_b%d" % r, [P, N], F32) for r in range(PACK)]
        mix = [tile("mix%d" % r, [P, N], F32) for r in range(PACK)]
        y = tile("y", [P, PACK, N], F32)
        y_bf = tile("y_bf", [P, N, PACK], BF16)
        y_codes = tile("y_codes", [P, N], U32)
        y_plane = tile("y_plane", [P, N], U8)

        nc.vector.memset(one[:], 1.0)
        for plane in (wc_plane, xs_plane_raw, ws_plane):
            nc.vector.memset(plane[:].bitcast(I32), 0)
        nc.scalar.activation(out=eps[:], in_=one[:], func=ACT.Square, scale=ROOT_EPS)

        make_identity(nc, ident[:])
        nc.gpsimd.memset(wa_plane[:].bitcast(I32), 0)
        for quad in range(QUADS):
            load_scale_rows(nc.gpsimd, wa_plane, wa_scales, quad)

        x_rows = xt.rearrange("(g p j) (h t) -> g h p j t", g=PASSES, j=PACK, h=HALVES)
        nc.sync.dma_start(out=gm_cols[:], in_=gm.rearrange("o (p j) -> (o p) j", j=PACK))
        nc.sync.dma_start(out=x_raw[0][0][:], in_=x_rows[0, 0])
        for quad in range(QUADS):
            load_scale_rows(nc.sync, wc_plane, wc_scales, quad, WC_ROW)
        nc.sync.dma_start(out=x_raw[0][1][:], in_=x_rows[0, 1])
        nc.sync.dma_start(out=wc_codes[0][:].bitcast(I32), in_=words_as_int32(wc_words[0]))
        nc.sync.dma_start(out=x_raw[1][0][:], in_=x_rows[1, 0])
        for quad in range(QUADS):
            load_scale_rows(nc.sync, xs_plane_raw, xs_scales, quad)
        nc.sync.dma_start(out=x_raw[1][1][:], in_=x_rows[1, 1])
        nc.sync.dma_start(out=wc_codes[1][:].bitcast(I32), in_=words_as_int32(wc_words[1]))
        nc.sync.dma_start(out=xs_codes_raw[:].bitcast(I32), in_=words_as_int32(xs_words[0]))
        nc.sync.dma_start(out=wa_codes[:].bitcast(I32), in_=wa_words.rearrange("g p c -> p g c").bitcast(I32))
        for quad in range(QUADS - 1):
            load_scale_rows(nc.sync, ws_plane, ws_scales, quad)
        nc.sync.dma_start(out=ws_codes[:].bitcast(I32), in_=ws_words[0].bitcast(I32))
        load_scale_rows(nc.sync, ws_plane, ws_scales, QUADS - 1)

        gm_bank = bank("a%d" % (PACK - 1))
        for j in range(PACK):
            nc.tensor.transpose(gm_bank[:, j * P : (j + 1) * P], gm_cols[:, j : j + 1].to_broadcast([P, P]), ident[:])

        def quantise_x(g, h):
            src = x_raw[g][h][:].rearrange("p j (q r) -> p q r j", r=PACK)
            dst = x_bf[g][h][:].rearrange("p r q j -> p q r j")
            nc.vector.tensor_copy(out=dst[:, :VECTOR_Q], in_=src[:, :VECTOR_Q])
            nc.scalar.copy(out=dst[:, VECTOR_Q:], in_=src[:, VECTOR_Q:])
            for r in range(PACK):
                cols = slice(r * P + h * HALF_Q, r * P + (h + 1) * HALF_Q)
                nc.vector.quantize_mx(
                    out=x_codes[g][:, cols].bitcast(FP8X4),
                    scales=x_plane[g][:, cols],
                    in_=x_bf[g][h][:, r].rearrange("p q j -> p (q j)"),
                )

        b = [bank("b%d" % r) for r in range(PACK)]

        def b_pass(r, g):
            nc.tensor.matmul_mx(
                out=b[r][:],
                lhsT=x_codes[g][:, hand(r)].bitcast(FP8X4),
                lhsT_scale=x_plane[g][:, hand(r)],
                rhs=wc_codes[g][:].bitcast(FP8X4),
                rhs_scale=wc_plane[WC_ROW:, g, :],
                start=(g == 0),
                stop=(g == PASSES - 1),
            )

        for h in range(HALVES):
            quantise_x(0, h)
        for r in range(PACK):
            b_pass(r, 0)
        for h in range(HALVES):
            quantise_x(1, h)

        nc.vector.tensor_copy(
            out=xs_plane[:].rearrange("p (r q) -> p r q", r=PACK),
            in_=xs_plane_raw[:, 0, :].rearrange("p (q r) -> p r q", r=PACK),
        )
        nc.vector.tensor_copy(
            out=xs_codes[:].bitcast(I32).rearrange("p (r q) -> p q r", r=PACK),
            in_=xs_codes_raw[:].bitcast(I32).rearrange("p (q r) -> p q r", r=PACK),
        )
        nc.scalar.copy(
            out=gm_rows[:].rearrange("p (c j) -> p c j", j=PACK), in_=gm_bank[:].rearrange("p (j c) -> p c j", j=PACK)
        )

        a = [bank("a%d" % r) for r in range(PACK)]

        def a_passes(r):
            for g in range(PASSES):
                nc.tensor.matmul_mx(
                    out=a[r][:],
                    lhsT=x_codes[g][:, hand(r)].bitcast(FP8X4),
                    lhsT_scale=x_plane[g][:, hand(r)],
                    rhs=wa_codes[:, g, :].bitcast(FP4X4),
                    rhs_scale=wa_plane[:, g, :],
                    start=(g == 0),
                    stop=False,
                )
            nc.tensor.matmul_mx(
                out=a[r][:],
                lhsT=xs_codes[:, hand(r)].bitcast(FP8X4),
                lhsT_scale=xs_plane[:, hand(r)],
                rhs=ws_codes[:].bitcast(FP4X4),
                rhs_scale=ws_plane[:, 0, :],
                start=False,
                stop=True,
            )

        for r in (0, 1, 2):
            b_pass(r, 1)
        for r in (0, 1):
            a_passes(r)
        b_pass(3, 1)
        for r in (2, 3):
            a_passes(r)

        def energy(acc, squares, e, r):
            nc.scalar.activation(
                out=squares[r][:], in_=acc[r][:], func=ACT.Square, scale=float(N) ** -0.5, accum_out=e[:, r : r + 1]
            )

        def mix_rows(r):
            col = slice(r, r + 1)
            nc.vector.tensor_scalar(
                out=den[:, col], in0=ea[:, col], scalar1=eb[:, col], scalar2=eps[:], op0=ALU.add, op1=ALU.add
            )
            nc.vector.scalar_tensor_tensor(
                out=mix[r][:], in0=a[r][:], scalar=ea[:, col], in1=eb_b[r][:], op0=ALU.mult, op1=ALU.add
            )
            nc.vector.reciprocal(out=inv[:, col], in_=den[:, col])

        def finish(r, cols):
            nc.vector.scalar_tensor_tensor(
                out=y[:, r, cols],
                in0=mix[r][:, cols],
                scalar=inv[:, r : r + 1],
                in1=gm_rows[:, cols],
                op0=ALU.mult,
                op1=ALU.mult,
            )

        def round_pair(copy, first_hand, cols):
            hands = slice(first_hand, first_hand + 2)
            copy(out=y_bf[:, cols, hands], in_=y[:, hands, cols].rearrange("p r n -> p n r"))

        y_rows = out_0.rearrange("(q r) n -> q r n", r=PACK)
        all_cols = slice(0, N)
        col_halves = (slice(0, N // 2), slice(N // 2, N))

        for r in (0, 1, 2):
            energy(b, b_squares, eb, r)
            nc.vector.tensor_scalar(out=eb_b[r][:], in0=b[r][:], scalar1=eb[:, r : r + 1], scalar2=None, op0=ALU.mult)
        for r in (0, 1):
            energy(a, a_squares, ea, r)
            mix_rows(r)
        energy(b, b_squares, eb, 3)
        energy(a, a_squares, ea, 2)
        for r in (0, 1):
            finish(r, all_cols)
            nc.sync.dma_start(out=y_rows[:, r, :], in_=y[:, r, :])
        mix_rows(2)
        nc.scalar.activation(out=eb_b[3][:], in_=b[3][:], func=ACT.Copy, scale=eb[:, 3:4])
        energy(a, a_squares, ea, 3)
        mix_rows(3)
        round_pair(nc.scalar.copy, 0, all_cols)
        for cols in col_halves:
            finish(2, cols)
            finish(3, cols)
            nc.sync.dma_start(out=y_rows[:, 2:4, cols], in_=y[:, 2:4, cols])
        round_pair(nc.scalar.copy, 2, col_halves[0])
        round_pair(nc.vector.tensor_copy, 2, col_halves[1])

        out_words = words_as_int32(out_1[0])
        for cols in col_halves:
            nc.vector.quantize_mx(
                out=y_codes[:, cols].bitcast(FP8X4),
                scales=y_plane[:, cols],
                in_=y_bf[:, cols, :].rearrange("p n r -> p (n r)"),
            )
            nc.sync.dma_start(out=out_words[:, cols], in_=y_codes[:, cols].bitcast(I32))
        for quad in range(QUADS):
            queue = nc.scalar if quad % 2 else nc.sync
            queue.dma_start(
                out=out_2[0, 4 * quad : 4 * quad + 4, :].bitcast(I32),
                in_=y_plane[32 * quad : 32 * quad + 4, :].bitcast(I32),
            )
